import numpy as np
import ml_dtypes


def mxq(x, axis, fmt="e4m3"):
    dtype, down = {"e4m3": (ml_dtypes.float8_e4m3fn, 7), "e5m2": (ml_dtypes.float8_e5m2, 14)}[fmt]
    v = np.moveaxis(np.asarray(x, np.float32).astype(ml_dtypes.bfloat16).astype(np.float64), axis, -1)
    blocks = v.reshape(v.shape[:-1] + (-1, 32))
    amax = np.abs(blocks).max(-1, keepdims=True)
    byte = np.maximum(np.where(amax > 0, np.frexp(amax)[1] - 1 + 127, 0) - down, 1)
    scale = np.exp2(byte - 127.0)
    codes = (blocks / scale).astype(np.float32).astype(dtype).astype(np.float64)
    return np.moveaxis((codes * scale).reshape(v.shape), -1, axis)


WIDE = False


def mx_kscale(k):
    if not WIDE:
        return np.ones(k)
    levels = np.array([10, -10, 5, -5, 0])
    if k % 512:
        return np.exp2(np.random.permutation(np.resize(levels, k // 32))).repeat(32)
    a = np.empty((k // 512, 16))
    for p in range(k // 512):
        a[p, :8] = np.random.permutation(np.resize(levels, 8))
        for g in range(8):
            far = levels[np.abs(levels - a[p, g]) >= 10]
            a[p, g + 8] = far[np.random.randint(len(far))]
    return np.exp2(a.ravel()).repeat(32)


def f64(x):
    return np.asarray(x).astype(np.float64)


def striped(idx):
    return np.tile(idx.reshape(-1, 16).T, (8, 1)).astype(np.uint16)


def unstriped(offs):
    return offs[:16].T.reshape(-1).astype(np.int64)


def pack_weight(w):
    k, n = w.shape
    w = f64(np.asarray(w, np.float32).astype(ml_dtypes.bfloat16)).reshape(k // 32, 32, n)
    amax = np.abs(w).max(1)
    byte = np.clip(np.where(amax > 0, np.frexp(amax)[1] - 1 + 127 - 7, 1), 1, 254)
    scaled = (w * np.exp2(127.0 - byte)[:, None, :]).reshape(k, n).astype(np.float32)
    words = np.ascontiguousarray(scaled.reshape(k // 512, 128, 4, n).transpose(0, 1, 3, 2)).astype(ml_dtypes.float8_e4m3fn).view(np.uint8)
    return words, np.ascontiguousarray(byte.astype(np.uint8).reshape(k // 512, 16, n))


def unpack_weight(words, scales):
    g, p, n, _ = words.shape
    vals = np.ascontiguousarray(words).view(ml_dtypes.float8_e4m3fn).astype(np.float64) * np.repeat(np.exp2(scales.astype(np.float64) - 127.0), 8, axis=1)[..., None]
    return vals.transpose(0, 1, 3, 2).reshape(g * 512, n)


def relu(v):
    return np.maximum(v, 0.0)


K, T, S, N = 1024, 1024, 512, 512


def setup_inputs():
    n = np.random.standard_normal
    s = mx_kscale(K)[:, None]
    w1, w2 = n((2, K, N)) / np.sqrt(2 * K) / s[None]
    packed = pack_weight(n((K, T)) * s)
    return {
        "xT": (n((K, S)) * s).astype(np.float32),
        "s_words": packed[0],
        "s_scales": packed[1],
        "w1": w1.astype(np.float32),
        "w2": w2.astype(np.float32),
        "b": (0.3 * n((N, 1))).astype(np.float32),
        "offs": striped(np.random.permutation(T)[:S]),
    }


def reference(xT, s_words, s_scales, w1, w2, b, offs):
    y = mxq(f64(w1), 0, "e4m3").T @ mxq(f64(xT), 0, "e4m3") + mxq(f64(w2), 0, "e4m3").T @ unpack_weight(s_words, s_scales)[:, unstriped(offs)]
    return relu(y + f64(b))

@@ -1,0 +1,151 @@
+from contextlib import ExitStack
+
+import concourse.mybir as mybir
+from concourse.masks import make_identity
+
+K, T, S, N = 1024, 1024, 512, 512
+FLOPS = 2 * 2 * K * N * S
+
+F32 = mybir.dt.float32
+BF16 = mybir.dt.bfloat16
+I32 = mybir.dt.int32
+U32 = mybir.dt.uint32
+U16 = mybir.dt.uint16
+U8 = mybir.dt.uint8
+FP8X4 = mybir.dt.float8_e4m3fn_x4
+ACT = mybir.ActivationFunctionType
+ALU = mybir.AluOpType
+
+P = 128
+PACK = 4
+K_PASS = P * PACK
+PASSES = K // K_PASS
+BLOCKS = N // P
+HALF = S // 2
+RUN = 4
+LAST_CUTS = ((0, 256), (256, 384), (384, 512))
+
+
+def tile_picked_recall_relu_p_kernel(tc, xT, s_words, s_scales, w1, w2, b, offs, out):
+    nc = tc.nc
+    with ExitStack() as ctx:
+        keep = ctx.enter_context(tc.tile_pool(name="keep", bufs=1))
+        stream = ctx.enter_context(tc.tile_pool(name="stream", bufs=4))
+        psum = ctx.enter_context(tc.psum_pool(name="psum", bufs=1))
+
+        def load_rows(matrix, o, cuts):
+            slot = stream.tile([P, PACK * N], F32, name="slot", align_bytes=64)
+            raws = []
+            for c0, c1 in cuts:
+                raw = slot[:, PACK * c0 : PACK * c1].rearrange("p (t c) -> p t c", t=PACK)
+                rows = matrix[o * K_PASS : (o + 1) * K_PASS, c0:c1]
+                nc.sync.dma_start(out=raw, in_=rows.rearrange("(p t) c -> p t c", t=PACK))
+                raws.append(raw)
+            return raws
+
+        def quantise(name, raw):
+            width = raw.shape[2]
+            half = width // 2
+            codes = keep.tile([P, width], U32, name=name + "_codes", align_bytes=64)
+            scales = keep.tile([P, width], U8, name=name + "_scales", align_bytes=64)
+            whole = width <= P
+            if whole:
+                one = keep.tile([P, width, PACK], BF16, name=name + "_bf", align_bytes=64)
+                shares = [one[:, :half, :], one[:, half:, :]]
+            else:
+                lo = keep.tile([P, half, PACK], BF16, name=name + "_lo", align_bytes=64)
+                hi = keep.tile([P, half, PACK], BF16, name=name + "_hi", align_bytes=64)
+                shares = [lo[:], hi[:]]
+            for h, copy in enumerate((nc.vector.tensor_copy, nc.scalar.copy)):
+                copy(
+                    out=shares[h].rearrange("p (c i) t -> p c t i", i=RUN),
+                    in_=raw[:, :, h * half : (h + 1) * half].rearrange("p t (c i) -> p c t i", i=RUN),
+                )
+            if whole:
+                nc.vector.quantize_mx(out=codes[:].bitcast(FP8X4), scales=scales[:], in_=one[:].rearrange("p c t -> p (c t)"))
+            else:
+                for h in range(2):
+                    cols = slice(h * half, (h + 1) * half)
+                    nc.vector.quantize_mx(
+                        out=codes[:, cols].bitcast(FP8X4),
+                        scales=scales[:, cols],
+                        in_=shares[h].rearrange("p c t -> p (c t)"),
+                    )
+            return codes, scales
+
+        identity = keep.tile([P, P], F32, name="identity", align_bytes=64)
+        make_identity(nc, identity[:])
+        scale_table = keep.tile([P, T], U8, name="scale_table", align_bytes=64)
+        nc.vector.memset(scale_table[:].bitcast(I32), 0)
+        bias_rows = keep.tile([P, P], F32, name="bias_rows", align_bytes=64)
+        nc.vector.memset(bias_rows[:], 0.0)
+        for q in range(4):
+            nc.gpsimd.dma_start(
+                out=scale_table[32 * q : 32 * q + 4 * PASSES, :].bitcast(I32),
+                in_=s_scales[:, 4 * q : 4 * q + 4, :].bitcast(I32),
+            )
+        nc.scalar.dma_start(out=bias_rows[0:BLOCKS, :], in_=b.rearrange("(c p) one -> c (p one)", p=P))
+
+        offsets = keep.tile([P, S // 16], U16, name="offsets")
+        word_tables = []
+        for o in range(PASSES):
+            table = keep.tile([P, T], I32, name=f"word_table{o}", align_bytes=64)
+            nc.sync.dma_start(out=table[:], in_=s_words[o].rearrange("p c t -> p (c t)").bitcast(I32))
+            word_tables.append(table)
+            if o == 0:
+                nc.sync.dma_start(offsets[:], offs)
+
+        acc = {}
+        bias_t = psum.tile([P, P], F32, name="bias_t", tag="bank7")
+        nc.tensor.transpose(bias_t[:], bias_rows[:], identity[:])
+        bias = keep.tile([P, BLOCKS], F32, name="bias")
+        nc.scalar.activation(out=bias[:], in_=bias_t[:, 0:BLOCKS], func=ACT.Copy)
+        for m in range(BLOCKS):
+            for h in range(2):
+                acc[m, h] = psum.tile([P, HALF], F32, name=f"acc{m}{h}", tag=f"bank{2 * m + h}")
+
+        picked_words = []
+        for o in range(PASSES):
+            words = keep.tile([P, S], U32, name=f"picked_words{o}", align_bytes=64)
+            nc.vector.tensor_copy(words[:], word_tables[o][:].bitcast(U32).indirect(offsets[:]))
+            picked_words.append(words)
+        picked_scales = keep.tile([P, S], U8, name="picked_scales", align_bytes=64)
+        nc.vector.tensor_copy(picked_scales[:], scale_table[:].indirect(offsets[:]))
+
+        x_mx = [quantise(f"x{o}", load_rows(xT, o, ((0, S),))[0]) for o in range(PASSES)]
+
+        for o, side in ((o, side) for o in range(PASSES) for side in range(2)):
+            first = o == 0 and side == 0
+            last = o == PASSES - 1 and side == 1
+            cuts = LAST_CUTS if last else ((0, N),)
+            for (c0, c1), raw in zip(cuts, load_rows((w1, w2)[side], o, cuts)):
+                codes, scales = quantise(f"w{o}{side}_{c0}", raw)
+                for m in range(c0 // P, c1 // P):
+                    cols = slice(m * P - c0, (m + 1) * P - c0)
+                    for h in range(2):
+                        q_cols = slice(h * HALF, (h + 1) * HALF)
+                        if side == 0:
+                            rhs, rhs_scale = x_mx[o][0][:, q_cols], x_mx[o][1][:, q_cols]
+                        else:
+                            rhs, rhs_scale = picked_words[o][:, q_cols], picked_scales[4 * o : P, q_cols]
+                        nc.tensor.matmul_mx(
+                            out=acc[m, h][:],
+                            lhsT=codes[:, cols].bitcast(FP8X4),
+                            lhsT_scale=scales[:, cols],
+                            rhs=rhs.bitcast(FP8X4),
+                            rhs_scale=rhs_scale,
+                            start=first,
+                            stop=last,
+                        )
+                    if last:
+                        result = keep.tile([P, S], F32, name=f"result{m}", align_bytes=64)
+                        nc.scalar.activation(out=result[:, :HALF], in_=acc[m, 0][:], func=ACT.Relu, bias=bias[:, m : m + 1])
+                        nc.vector.tensor_scalar(
+                            out=result[:, HALF:],
+                            in0=acc[m, 1][:],
+                            scalar1=bias[:, m : m + 1],
+                            scalar2=0.0,
+                            op0=ALU.add,
+                            op1=ALU.max,
+                        )
+                        nc.sync.dma_start(out=out[m * P : (m + 1) * P, :], in_=result[:])

@@ -30,7 +30,7 @@ def tile_picked_recall_relu_p_kernel(tc, xT, s_words, s_scales, w1, w2, b, offs,
     nc = tc.nc
     with ExitStack() as ctx:
         keep = ctx.enter_context(tc.tile_pool(name="keep", bufs=1))
-        stream = ctx.enter_context(tc.tile_pool(name="stream", bufs=4))
+        stream = ctx.enter_context(tc.tile_pool(name="stream", bufs=6))
         psum = ctx.enter_context(tc.psum_pool(name="psum", bufs=1))
 
         def load_rows(matrix, o, cuts):
@@ -73,27 +73,28 @@ def tile_picked_recall_relu_p_kernel(tc, xT, s_words, s_scales, w1, w2, b, offs,
                     )
             return codes, scales
 
-        identity = keep.tile([P, P], F32, name="identity", align_bytes=64)
-        make_identity(nc, identity[:])
         scale_table = keep.tile([P, T], U8, name="scale_table", align_bytes=64)
         nc.vector.memset(scale_table[:].bitcast(I32), 0)
         bias_rows = keep.tile([P, P], F32, name="bias_rows", align_bytes=64)
         nc.vector.memset(bias_rows[:], 0.0)
+        identity = keep.tile([P, P], F32, name="identity", align_bytes=64)
+        make_identity(nc, identity[:])
+
+        word_table = keep.tile([P, PASSES * T], I32, name="word_table", align_bytes=64)
+        nc.sync.dma_start(
+            out=word_table[:].rearrange("p (o c) -> p o c", o=PASSES),
+            in_=s_words.rearrange("o p c t -> p o (c t)").bitcast(I32),
+        )
+        offsets = keep.tile([P, S // 16], U16, name="offsets")
+        nc.sync.dma_start(offsets[:], offs)
+        x_raw = [load_rows(xT, 0, ((0, S),))[0]]
         for q in range(4):
-            nc.gpsimd.dma_start(
+            nc.sync.dma_start(
                 out=scale_table[32 * q : 32 * q + 4 * PASSES, :].bitcast(I32),
                 in_=s_scales[:, 4 * q : 4 * q + 4, :].bitcast(I32),
             )
-        nc.scalar.dma_start(out=bias_rows[0:BLOCKS, :], in_=b.rearrange("(c p) one -> c (p one)", p=P))
-
-        offsets = keep.tile([P, S // 16], U16, name="offsets")
-        word_tables = []
-        for o in range(PASSES):
-            table = keep.tile([P, T], I32, name=f"word_table{o}", align_bytes=64)
-            nc.sync.dma_start(out=table[:], in_=s_words[o].rearrange("p c t -> p (c t)").bitcast(I32))
-            word_tables.append(table)
-            if o == 0:
-                nc.sync.dma_start(offsets[:], offs)
+        nc.sync.dma_start(out=bias_rows[0:BLOCKS, :], in_=b.rearrange("(c p) one -> c (p one)", p=P))
+        x_raw.append(load_rows(xT, 1, ((0, S),))[0])
 
         acc = {}
         bias_t = psum.tile([P, P], F32, name="bias_t", tag="bank7")
@@ -107,12 +108,12 @@ def tile_picked_recall_relu_p_kernel(tc, xT, s_words, s_scales, w1, w2, b, offs,
         picked_words = []
         for o in range(PASSES):
             words = keep.tile([P, S], U32, name=f"picked_words{o}", align_bytes=64)
-            nc.vector.tensor_copy(words[:], word_tables[o][:].bitcast(U32).indirect(offsets[:]))
+            nc.vector.tensor_copy(words[:], word_table[:, o * T : (o + 1) * T].bitcast(U32).indirect(offsets[:]))
             picked_words.append(words)
         picked_scales = keep.tile([P, S], U8, name="picked_scales", align_bytes=64)
         nc.vector.tensor_copy(picked_scales[:], scale_table[:].indirect(offsets[:]))
 
-        x_mx = [quantise(f"x{o}", load_rows(xT, o, ((0, S),))[0]) for o in range(PASSES)]
+        x_mx = [quantise(f"x{o}", x_raw[o]) for o in range(PASSES)]
 
         for o, side in ((o, side) for o in range(PASSES) for side in range(2)):
             first = o == 0 and side == 0

from contextlib import ExitStack

import concourse.mybir as mybir
from concourse.masks import make_identity

K, T, S, N = 1024, 1024, 512, 512
FLOPS = 2 * 2 * K * N * S

F32 = mybir.dt.float32
BF16 = mybir.dt.bfloat16
I32 = mybir.dt.int32
U32 = mybir.dt.uint32
U16 = mybir.dt.uint16
U8 = mybir.dt.uint8
FP8X4 = mybir.dt.float8_e4m3fn_x4
ACT = mybir.ActivationFunctionType
ALU = mybir.AluOpType

P = 128
PACK = 4
K_PASS = P * PACK
PASSES = K // K_PASS
BLOCKS = N // P
HALF = S // 2
RUN = 4
LAST_CUTS = ((0, 256), (256, 384), (384, 512))


def tile_picked_recall_relu_p_kernel(tc, xT, s_words, s_scales, w1, w2, b, offs, out):
    nc = tc.nc
    with ExitStack() as ctx:
        keep = ctx.enter_context(tc.tile_pool(name="keep", bufs=1))
        stream = ctx.enter_context(tc.tile_pool(name="stream", bufs=6))
        psum = ctx.enter_context(tc.psum_pool(name="psum", bufs=1))

        def load_rows(matrix, o, cuts):
            slot = stream.tile([P, PACK * N], F32, name="slot", align_bytes=64)
            raws = []
            for c0, c1 in cuts:
                raw = slot[:, PACK * c0 : PACK * c1].rearrange("p (t c) -> p t c", t=PACK)
                rows = matrix[o * K_PASS : (o + 1) * K_PASS, c0:c1]
                nc.sync.dma_start(out=raw, in_=rows.rearrange("(p t) c -> p t c", t=PACK))
                raws.append(raw)
            return raws

        def quantise(name, raw):
            width = raw.shape[2]
            half = width // 2
            codes = keep.tile([P, width], U32, name=name + "_codes", align_bytes=64)
            scales = keep.tile([P, width], U8, name=name + "_scales", align_bytes=64)
            whole = width <= P
            if whole:
                one = keep.tile([P, width, PACK], BF16, name=name + "_bf", align_bytes=64)
                shares = [one[:, :half, :], one[:, half:, :]]
            else:
                lo = keep.tile([P, half, PACK], BF16, name=name + "_lo", align_bytes=64)
                hi = keep.tile([P, half, PACK], BF16, name=name + "_hi", align_bytes=64)
                shares = [lo[:], hi[:]]
            for h, copy in enumerate((nc.vector.tensor_copy, nc.scalar.copy)):
                copy(
                    out=shares[h].rearrange("p (c i) t -> p c t i", i=RUN),
                    in_=raw[:, :, h * half : (h + 1) * half].rearrange("p t (c i) -> p c t i", i=RUN),
                )
            if whole:
                nc.vector.quantize_mx(out=codes[:].bitcast(FP8X4), scales=scales[:], in_=one[:].rearrange("p c t -> p (c t)"))
            else:
                for h in range(2):
                    cols = slice(h * half, (h + 1) * half)
                    nc.vector.quantize_mx(
                        out=codes[:, cols].bitcast(FP8X4),
                        scales=scales[:, cols],
                        in_=shares[h].rearrange("p c t -> p (c t)"),
                    )
            return codes, scales

        scale_table = keep.tile([P, T], U8, name="scale_table", align_bytes=64)
        nc.vector.memset(scale_table[:].bitcast(I32), 0)
        bias_rows = keep.tile([P, P], F32, name="bias_rows", align_bytes=64)
        nc.vector.memset(bias_rows[:], 0.0)
        identity = keep.tile([P, P], F32, name="identity", align_bytes=64)
        make_identity(nc, identity[:])

        word_table = keep.tile([P, PASSES * T], I32, name="word_table", align_bytes=64)
        nc.sync.dma_start(
            out=word_table[:].rearrange("p (o c) -> p o c", o=PASSES),
            in_=s_words.rearrange("o p c t -> p o (c t)").bitcast(I32),
        )
        offsets = keep.tile([P, S // 16], U16, name="offsets")
        nc.sync.dma_start(offsets[:], offs)
        x_raw = [load_rows(xT, 0, ((0, S),))[0]]
        for q in range(4):
            nc.sync.dma_start(
                out=scale_table[32 * q : 32 * q + 4 * PASSES, :].bitcast(I32),
                in_=s_scales[:, 4 * q : 4 * q + 4, :].bitcast(I32),
            )
        nc.sync.dma_start(out=bias_rows[0:BLOCKS, :], in_=b.rearrange("(c p) one -> c (p one)", p=P))
        x_raw.append(load_rows(xT, 1, ((0, S),))[0])

        acc = {}
        bias_t = psum.tile([P, P], F32, name="bias_t", tag="bank7")
        nc.tensor.transpose(bias_t[:], bias_rows[:], identity[:])
        bias = keep.tile([P, BLOCKS], F32, name="bias")
        nc.scalar.activation(out=bias[:], in_=bias_t[:, 0:BLOCKS], func=ACT.Copy)
        for m in range(BLOCKS):
            for h in range(2):
                acc[m, h] = psum.tile([P, HALF], F32, name=f"acc{m}{h}", tag=f"bank{2 * m + h}")

        picked_words = []
        for o in range(PASSES):
            words = keep.tile([P, S], U32, name=f"picked_words{o}", align_bytes=64)
            nc.vector.tensor_copy(words[:], word_table[:, o * T : (o + 1) * T].bitcast(U32).indirect(offsets[:]))
            picked_words.append(words)
        picked_scales = keep.tile([P, S], U8, name="picked_scales", align_bytes=64)
        nc.vector.tensor_copy(picked_scales[:], scale_table[:].indirect(offsets[:]))

        x_mx = [quantise(f"x{o}", x_raw[o]) for o in range(PASSES)]

        for o, side in ((o, side) for o in range(PASSES) for side in range(2)):
            first = o == 0 and side == 0
            last = o == PASSES - 1 and side == 1
            cuts = LAST_CUTS if last else ((0, N),)
            for (c0, c1), raw in zip(cuts, load_rows((w1, w2)[side], o, cuts)):
                codes, scales = quantise(f"w{o}{side}_{c0}", raw)
                for m in range(c0 // P, c1 // P):
                    cols = slice(m * P - c0, (m + 1) * P - c0)
                    for h in range(2):
                        q_cols = slice(h * HALF, (h + 1) * HALF)
                        if side == 0:
                            rhs, rhs_scale = x_mx[o][0][:, q_cols], x_mx[o][1][:, q_cols]
                        else:
                            rhs, rhs_scale = picked_words[o][:, q_cols], picked_scales[4 * o : P, q_cols]
                        nc.tensor.matmul_mx(
                            out=acc[m, h][:],
                            lhsT=codes[:, cols].bitcast(FP8X4),
                            lhsT_scale=scales[:, cols],
                            rhs=rhs.bitcast(FP8X4),
                            rhs_scale=rhs_scale,
                            start=first,
                            stop=last,
                        )
                    if last:
                        result = keep.tile([P, S], F32, name=f"result{m}", align_bytes=64)
                        nc.scalar.activation(out=result[:, :HALF], in_=acc[m, 0][:], func=ACT.Relu, bias=bias[:, m : m + 1])
                        nc.vector.tensor_scalar(
                            out=result[:, HALF:],
                            in0=acc[m, 1][:],
                            scalar1=bias[:, m : m + 1],
                            scalar2=0.0,
                            op0=ALU.add,
                            op1=ALU.max,
                        )
                        nc.sync.dma_start(out=out[m * P : (m + 1) * P, :], in_=result[:])
